import numpy as np
import ml_dtypes


def mxq(x, axis, fmt="e4m3"):
    dtype, down = {"e4m3": (ml_dtypes.float8_e4m3fn, 7), "e5m2": (ml_dtypes.float8_e5m2, 14)}[fmt]
    v = np.moveaxis(np.asarray(x, np.float32).astype(ml_dtypes.bfloat16).astype(np.float64), axis, -1)
    blocks = v.reshape(v.shape[:-1] + (-1, 32))
    amax = np.abs(blocks).max(-1, keepdims=True)
    byte = np.maximum(np.where(amax > 0, np.frexp(amax)[1] - 1 + 127, 0) - down, 1)
    scale = np.exp2(byte - 127.0)
    codes = (blocks / scale).astype(np.float32).astype(dtype).astype(np.float64)
    return np.moveaxis((codes * scale).reshape(v.shape), -1, axis)


WIDE = False


def mx_kscale(k):
    if not WIDE:
        return np.ones(k)
    levels = np.array([30, -30])
    if k % 512:
        return np.exp2(np.random.permutation(np.resize(levels, k // 32))).repeat(32)
    a = np.empty((k // 512, 16))
    for p in range(k // 512):
        a[p, :8] = np.random.permutation(np.resize(levels, 8))
        for g in range(8):
            far = levels[np.abs(levels - a[p, g]) >= 10]
            a[p, g + 8] = far[np.random.randint(len(far))]
    return np.exp2(a.ravel()).repeat(32)


def f64(x):
    return np.asarray(x).astype(np.float64)


K, M, T = 2048, 512, 1536


def setup_inputs():
    n = np.random.standard_normal
    s1 = mx_kscale(K)[:, None]
    s2 = mx_kscale(K)[:, None]
    return {
        "w": (n((K, M)) / np.sqrt(K) * s1).astype(np.float32),
        "xd": (n((K, T)) / s1).astype(np.float32),
        "wd": (n((K, M)) / np.sqrt(K) * s2).astype(np.float32),
        "x": (n((K, T)) / s2).astype(np.float32),
        "b": (0.3 * n(512)).astype(np.float32),
    }


def reference(w, xd, wd, x, b):
    w_ = mxq(f64(w), 0, "e4m3")
    xd_ = mxq(f64(xd), 0, "e5m2")
    wd_ = mxq(f64(wd), 0, "e5m2")
    x_ = mxq(f64(x), 0, "e4m3")
    y = w_.T @ xd_ + wd_.T @ x_
    return y + f64(b)[:, None]

@@ -1,0 +1,198 @@
+from contextlib import ExitStack
+
+import concourse.mybir as mybir
+
+K, M, T = 2048, 512, 1536
+FLOPS = 2 * 2 * K * M * T
+
+F32 = mybir.dt.float32
+BF16 = mybir.dt.bfloat16
+U32 = mybir.dt.uint32
+U8 = mybir.dt.uint8
+E4M3 = mybir.dt.float8_e4m3fn_x4
+E5M2 = mybir.dt.float8_e5m2_x4
+IDENTITY = mybir.ActivationFunctionType.Identity
+ADD = mybir.AluOpType.add
+
+P = 128
+PACK = 4
+K_PASS = P * PACK
+N = 512
+M_TILES = M // P
+RANGES = T // N
+CHUNKS = 2 * K // K_PASS
+SPILL = 6
+V_COLS = 336
+
+
+def tile_mix_jvp_fm_bias_kernel(tc, w, xd, wd, x, b, out):
+    nc = tc.nc
+
+    with ExitStack() as ctx:
+        const = ctx.enter_context(tc.tile_pool(name="const", bufs=1))
+        wide = ctx.enter_context(tc.tile_pool(name="wide", bufs=3))
+        narrow = ctx.enter_context(tc.tile_pool(name="narrow", bufs=4))
+        group = ctx.enter_context(tc.tile_pool(name="group", bufs=5))
+        banks = ctx.enter_context(tc.psum_pool(name="banks", bufs=1))
+        ctx.enter_context(tc.manual_schedule())
+
+        w_codes = const.tile([P, CHUNKS, M], U32, align_bytes=64)
+        w_scales = const.tile([P, CHUNKS, M], U8, align_bytes=64)
+        x_codes = const.tile([P, CHUNKS, RANGES, N], U32, align_bytes=64)
+        x_scales = const.tile([P, CHUNKS, RANGES, N], U8, align_bytes=64)
+        results = const.tile([P, RANGES, M_TILES, N], F32, align_bytes=64)
+        bias_rows = const.tile([P, 32], F32, align_bytes=64)
+        bias = const.tile([P, 32], F32, align_bytes=64)
+
+        def operands(c):
+            g = c // 2
+            rows = slice(g * K_PASS, (g + 1) * K_PASS)
+            if c % 2 == 0:
+                return w[rows, :], E4M3, xd[rows, :], E5M2
+            return wd[rows, :], E5M2, x[rows, :], E4M3
+
+        def load_narrow(src):
+            raw = narrow.tile([P, PACK, N], F32, name="raw", align_bytes=64)
+            nc.sync.dma_start(out=raw[:], in_=src.rearrange("(p j) c -> p j c", j=PACK))
+            return raw
+
+        def load_wide(src):
+            raw_wide = wide.tile([P, PACK, T], F32, name="raw_wide", align_bytes=64)
+            nc.sync.dma_start(out=raw_wide[:], in_=src.rearrange("(p j) c -> p j c", j=PACK))
+            return raw_wide
+
+        def interleave(copy, grouped, raw, c0, c1):
+            copy(
+                out=grouped[:, c0:c1, :].rearrange("p (c i) t -> p c t i", i=4),
+                in_=raw[:, :, c0:c1].rearrange("p t (c i) -> p c t i", i=4),
+            )
+
+        def cast(raw, v_cols):
+            grouped = group.tile([P, N, PACK], BF16, name="grouped", align_bytes=64)
+            if v_cols < N:
+                interleave(nc.scalar.copy, grouped, raw, v_cols, N)
+            if v_cols > 0:
+                interleave(nc.vector.tensor_copy, grouped, raw, 0, v_cols)
+            return grouped
+
+        def quantize(grouped, codes, scales, fmt):
+            nc.vector.quantize_mx(
+                out=codes.bitcast(fmt), scales=scales, in_=grouped[:].rearrange("p c t -> p (c t)")
+            )
+
+        def quantize_w(c, grouped):
+            quantize(grouped, w_codes[:, c, :], w_scales[:, c, :], operands(c)[1])
+
+        def quantize_x(c, r, grouped):
+            quantize(grouped, x_codes[:, c, r, :], x_scales[:, c, r, :], operands(c)[3])
+
+        acc = {}
+
+        def open_bank(r, m, bank):
+            acc[r, m] = banks.tile([P, N], F32, name="bank" + str(bank))
+
+        def multiply(c, r, m, start, stop):
+            cols = slice(m * P, (m + 1) * P)
+            nc.tensor.matmul_mx(
+                out=acc[r, m][:],
+                lhsT=w_codes[:, c, cols].bitcast(operands(c)[1]),
+                lhsT_scale=w_scales[:, c, cols],
+                rhs=x_codes[:, c, r, :].bitcast(operands(c)[3]),
+                rhs_scale=x_scales[:, c, r, :],
+                start=start,
+                stop=stop,
+            )
+
+        def add_bias(r, m, on_vector):
+            if on_vector:
+                nc.vector.tensor_scalar(
+                    out=results[:, r, m, :], in0=acc[r, m][:], scalar1=bias[:, m : m + 1], scalar2=None, op0=ADD
+                )
+            else:
+                nc.scalar.activation(
+                    out=results[:, r, m, :], in_=acc[r, m][:], func=IDENTITY, bias=bias[:, m : m + 1]
+                )
+
+        def store(r, m):
+            nc.sync.dma_start(out=out[m * P : (m + 1) * P, r * N : (r + 1) * N], in_=results[:, r, m, :])
+
+        nc.vector.memset(bias_rows[:], 0.0)
+        for m in range(M_TILES):
+            nc.gpsimd.dma_start(
+                out=bias_rows[m : P : 32, :], in_=b[m * P : (m + 1) * P].rearrange("(q i) -> q i", i=32)
+            )
+        nc.vector.transpose(bias[:], bias_rows[:])
+
+        raw_w, raw_x = {}, {}
+        for c in range(CHUNKS - 2):
+            raw_w[c] = load_narrow(operands(c)[0])
+            raw_x[c] = load_wide(operands(c)[2])
+            quantize_w(c, cast(raw_w[c], 0))
+            pieces = {}
+            for r in range(RANGES):
+                pieces[r] = cast(raw_x[c][:, :, r * N : (r + 1) * N], V_COLS)
+                if r > 0:
+                    quantize_x(c, r - 1, pieces[r - 1])
+            quantize_x(c, RANGES - 1, pieces[RANGES - 1])
+            for r in range(2):
+                for m in range(M_TILES):
+                    if c == 0:
+                        open_bank(r, m, 4 * r + m)
+                    multiply(c, r, m, c == 0, r == 1 and c == SPILL - 1)
+
+        last = CHUNKS - 1
+        before = CHUNKS - 2
+        raw_w[before] = load_narrow(operands(before)[0])
+        raw_w[last] = load_narrow(operands(last)[0])
+        raw_x[before] = load_wide(operands(before)[2])
+
+        quantize_w(before, cast(raw_w[before], 0))
+        quantize_w(last, cast(raw_w[last], 0))
+        tail = [load_narrow(operands(last)[2][:, r * N : (r + 1) * N]) for r in range(RANGES)]
+
+        for m in range(M_TILES):
+            add_bias(1, m, m % 2 == 1)
+            open_bank(2, m, 4 + m)
+            for c in range(SPILL):
+                multiply(c, 2, m, c == 0, False)
+
+        pieces = {}
+        for r in range(RANGES):
+            pieces[r] = cast(raw_x[before][:, :, r * N : (r + 1) * N], V_COLS)
+            if r > 0:
+                quantize_x(before, r - 1, pieces[r - 1])
+        quantize_x(before, RANGES - 1, pieces[RANGES - 1])
+        for r in (0, 2):
+            for m in range(M_TILES):
+                multiply(before, r, m, False, False)
+
+        quantize_x(last, 0, cast(tail[0], V_COLS))
+        for m in range(M_TILES):
+            multiply(last, 0, m, False, True)
+        for m in range(M_TILES):
+            add_bias(0, m, m % 2 == 1)
+            store(0, m)
+            open_bank(1, m, m)
+            multiply(before, 1, m, True, False)
+
+        quantize_x(last, 1, cast(tail[1], V_COLS))
+        for m in range(M_TILES):
+            multiply(last, 1, m, False, True)
+
+        def add_partial(m):
+            nc.vector.tensor_tensor(
+                out=results[:, 1, m, :], in0=acc[1, m][:], in1=results[:, 1, m, :], op=ADD
+            )
+            store(1, m)
+
+        add_partial(0)
+        final = cast(tail[2], V_COLS)
+        add_partial(1)
+        quantize_x(last, 2, final)
+        for m in range(M_TILES):
+            multiply(last, 2, m, False, True)
+        add_partial(2)
+        add_partial(3)
+        for m in range(M_TILES):
+            add_bias(2, m, m % 2 == 1)
+            store(2, m)

@@ -21,7 +21,7 @@ N = 512
 M_TILES = M // P
 RANGES = T // N
 CHUNKS = 2 * K // K_PASS
-SPILL = 6
+SPILL = 5
 V_COLS = 336
 
 
@@ -57,7 +57,7 @@ def tile_mix_jvp_fm_bias_kernel(tc, w, xd, wd, x, b, out):
             return raw
 
         def load_wide(src):
-            raw_wide = wide.tile([P, PACK, T], F32, name="raw_wide", align_bytes=64)
+            raw_wide = wide.tile([P, PACK, src.shape[1]], F32, name="raw_wide", align_bytes=64)
             nc.sync.dma_start(out=raw_wide[:], in_=src.rearrange("(p j) c -> p j c", j=PACK))
             return raw_wide
 
@@ -118,81 +118,89 @@ def tile_mix_jvp_fm_bias_kernel(tc, w, xd, wd, x, b, out):
 
         nc.vector.memset(bias_rows[:], 0.0)
         for m in range(M_TILES):
-            nc.gpsimd.dma_start(
+            nc.scalar.dma_start(
                 out=bias_rows[m : P : 32, :], in_=b[m * P : (m + 1) * P].rearrange("(q i) -> q i", i=32)
             )
-        nc.vector.transpose(bias[:], bias_rows[:])
 
-        raw_w, raw_x = {}, {}
+        def finish(r, m, on_vector):
+            add_bias(r, m, on_vector)
+            store(r, m)
+
+        def finish_partial(r, m):
+            nc.vector.tensor_tensor(
+                out=results[:, r, m, :], in0=acc[r, m][:], in1=results[:, r, m, :], op=ADD
+            )
+            store(r, m)
+
+        def piece(raw, i):
+            return raw[:, :, i * N : (i + 1) * N]
+
+        early, split, late = 0, 1, 2
         for c in range(CHUNKS - 2):
-            raw_w[c] = load_narrow(operands(c)[0])
-            raw_x[c] = load_wide(operands(c)[2])
-            quantize_w(c, cast(raw_w[c], 0))
-            pieces = {}
-            for r in range(RANGES):
-                pieces[r] = cast(raw_x[c][:, :, r * N : (r + 1) * N], V_COLS)
-                if r > 0:
-                    quantize_x(c, r - 1, pieces[r - 1])
-            quantize_x(c, RANGES - 1, pieces[RANGES - 1])
-            for r in range(2):
+            raw_w = load_narrow(operands(c)[0])
+            raw_x = load_wide(operands(c)[2])
+            quantize_w(c, cast(raw_w, 0))
+            grouped_x = [cast(piece(raw_x, 0), V_COLS), cast(piece(raw_x, 1), V_COLS)]
+            quantize_x(c, 0, grouped_x[0])
+            grouped_x.append(cast(piece(raw_x, 2), V_COLS))
+            quantize_x(c, 1, grouped_x[1])
+            quantize_x(c, 2, grouped_x[2])
+            for r, bank in ((late, 0), (split if c < SPILL else early, 4)):
                 for m in range(M_TILES):
                     if c == 0:
-                        open_bank(r, m, 4 * r + m)
-                    multiply(c, r, m, c == 0, r == 1 and c == SPILL - 1)
+                        open_bank(r, m, bank + m)
+                    multiply(c, r, m, c == 0, r == split and c == SPILL - 1)
+            if c == SPILL - 1:
+                nc.vector.transpose(bias[:], bias_rows[:])
+                for m in range(M_TILES):
+                    add_bias(split, m, m % 2 == 1)
+                    open_bank(early, m, 4 + m)
+                    for done in range(SPILL):
+                        multiply(done, early, m, done == 0, False)
 
-        last = CHUNKS - 1
-        before = CHUNKS - 2
-        raw_w[before] = load_narrow(operands(before)[0])
-        raw_w[last] = load_narrow(operands(last)[0])
-        raw_x[before] = load_wide(operands(before)[2])
+        c6, c7 = CHUNKS - 2, CHUNKS - 1
+        x6, x7 = operands(c6)[2], operands(c7)[2]
 
-        quantize_w(before, cast(raw_w[before], 0))
-        quantize_w(last, cast(raw_w[last], 0))
-        tail = [load_narrow(operands(last)[2][:, r * N : (r + 1) * N]) for r in range(RANGES)]
+        def columns(src, r):
+            return src[:, r * N : (r + 1) * N]
 
+        raw_w6 = load_narrow(operands(c6)[0])
+        raw_w7 = load_narrow(operands(c7)[0])
+        raw_early6 = load_narrow(columns(x6, early))
+        raw_early7 = load_narrow(columns(x7, early))
+        quantize_w(c6, cast(raw_w6, 0))
+        quantize_w(c7, cast(raw_w7, 0))
+        raw_rest6 = load_wide(x6[:, N:])
+        raw_split7 = load_narrow(columns(x7, split))
+        raw_late7 = load_narrow(columns(x7, late))
+
+        quantize_x(c6, early, cast(raw_early6, V_COLS))
         for m in range(M_TILES):
-            add_bias(1, m, m % 2 == 1)
-            open_bank(2, m, 4 + m)
-            for c in range(SPILL):
-                multiply(c, 2, m, c == 0, False)
+            multiply(c6, early, m, False, False)
+        quantize_x(c7, early, cast(raw_early7, V_COLS))
+        for m in range(M_TILES):
+            multiply(c7, early, m, False, True)
+        for m in range(M_TILES):
+            finish(early, m, m % 2 == 1)
+            open_bank(split, m, 4 + m)
+            for c in range(SPILL, c6):
+                multiply(c, split, m, c == SPILL, False)
 
-        pieces = {}
-        for r in range(RANGES):
-            pieces[r] = cast(raw_x[before][:, :, r * N : (r + 1) * N], V_COLS)
-            if r > 0:
-                quantize_x(before, r - 1, pieces[r - 1])
-        quantize_x(before, RANGES - 1, pieces[RANGES - 1])
-        for r in (0, 2):
+        grouped_split = cast(piece(raw_rest6, 0), V_COLS)
+        grouped_late = cast(piece(raw_rest6, 1), V_COLS)
+        quantize_x(c6, split, grouped_split)
+        quantize_x(c6, late, grouped_late)
+        for r in (split, late):
             for m in range(M_TILES):
-                multiply(before, r, m, False, False)
+                multiply(c6, r, m, False, False)
 
-        quantize_x(last, 0, cast(tail[0], V_COLS))
+        quantize_x(c7, split, cast(raw_split7, V_COLS))
         for m in range(M_TILES):
-            multiply(last, 0, m, False, True)
+            multiply(c7, split, m, False, True)
+        quantize_x(c7, late, cast(raw_late7, V_COLS))
         for m in range(M_TILES):
-            add_bias(0, m, m % 2 == 1)
-            store(0, m)
-            open_bank(1, m, m)
-            multiply(before, 1, m, True, False)
-
-        quantize_x(last, 1, cast(tail[1], V_COLS))
+            multiply(c7, late, m, False, True)
         for m in range(M_TILES):
-            multiply(last, 1, m, False, True)
-
-        def add_partial(m):
-            nc.vector.tensor_tensor(
-                out=results[:, 1, m, :], in0=acc[1, m][:], in1=results[:, 1, m, :], op=ADD
-            )
-            store(1, m)
-
-        add_partial(0)
-        final = cast(tail[2], V_COLS)
-        add_partial(1)
-        quantize_x(last, 2, final)
+            finish_partial(split, m)
         for m in range(M_TILES):
-            multiply(last, 2, m, False, True)
-        add_partial(2)
-        add_partial(3)
-        for m in range(M_TILES):
-            add_bias(2, m, m % 2 == 1)
-            store(2, m)
+            finish(late, m, m == M_TILES - 1)

@@ -21,7 +21,7 @@ N = 512
 M_TILES = M // P
 RANGES = T // N
 CHUNKS = 2 * K // K_PASS
-SPILL = 5
+WHOLE = 5
 V_COLS = 336
 
 
@@ -30,9 +30,9 @@ def tile_mix_jvp_fm_bias_kernel(tc, w, xd, wd, x, b, out):
 
     with ExitStack() as ctx:
         const = ctx.enter_context(tc.tile_pool(name="const", bufs=1))
-        wide = ctx.enter_context(tc.tile_pool(name="wide", bufs=3))
-        narrow = ctx.enter_context(tc.tile_pool(name="narrow", bufs=4))
-        group = ctx.enter_context(tc.tile_pool(name="group", bufs=5))
+        wide = ctx.enter_context(tc.tile_pool(name="wide", bufs=2))
+        narrow = ctx.enter_context(tc.tile_pool(name="narrow", bufs=6))
+        group = ctx.enter_context(tc.tile_pool(name="group", bufs=6))
         banks = ctx.enter_context(tc.psum_pool(name="banks", bufs=1))
         ctx.enter_context(tc.manual_schedule())
 
@@ -126,81 +126,80 @@ def tile_mix_jvp_fm_bias_kernel(tc, w, xd, wd, x, b, out):
             add_bias(r, m, on_vector)
             store(r, m)
 
-        def finish_partial(r, m):
-            nc.vector.tensor_tensor(
-                out=results[:, r, m, :], in0=acc[r, m][:], in1=results[:, r, m, :], op=ADD
-            )
-            store(r, m)
-
         def piece(raw, i):
             return raw[:, :, i * N : (i + 1) * N]
 
         early, split, late = 0, 1, 2
-        for c in range(CHUNKS - 2):
-            raw_w = load_narrow(operands(c)[0])
+        AHEAD = 3
+        raw_w = [load_narrow(operands(c)[0]) for c in range(AHEAD)]
+        for c in range(WHOLE):
+            raw_w.append(load_narrow(operands(c + AHEAD)[0]))
             raw_x = load_wide(operands(c)[2])
-            quantize_w(c, cast(raw_w, 0))
+            for ready in range(0 if c == 0 else c + AHEAD, c + AHEAD + 1):
+                quantize_w(ready, cast(raw_w[ready], 0))
             grouped_x = [cast(piece(raw_x, 0), V_COLS), cast(piece(raw_x, 1), V_COLS)]
             quantize_x(c, 0, grouped_x[0])
             grouped_x.append(cast(piece(raw_x, 2), V_COLS))
             quantize_x(c, 1, grouped_x[1])
             quantize_x(c, 2, grouped_x[2])
-            for r, bank in ((late, 0), (split if c < SPILL else early, 4)):
+            for r, bank in ((late, 0), (early, 4)):
                 for m in range(M_TILES):
                     if c == 0:
                         open_bank(r, m, bank + m)
-                    multiply(c, r, m, c == 0, r == split and c == SPILL - 1)
-            if c == SPILL - 1:
-                nc.vector.transpose(bias[:], bias_rows[:])
-                for m in range(M_TILES):
-                    add_bias(split, m, m % 2 == 1)
-                    open_bank(early, m, 4 + m)
-                    for done in range(SPILL):
-                        multiply(done, early, m, done == 0, False)
+                    multiply(c, r, m, c == 0, False)
 
-        c6, c7 = CHUNKS - 2, CHUNKS - 1
-        x6, x7 = operands(c6)[2], operands(c7)[2]
+        nc.vector.transpose(bias[:], bias_rows[:])
 
-        def columns(src, r):
-            return src[:, r * N : (r + 1) * N]
+        def columns(c, r0, r1):
+            return operands(c)[2][:, r0 * N : r1 * N]
 
-        raw_w6 = load_narrow(operands(c6)[0])
-        raw_w7 = load_narrow(operands(c7)[0])
-        raw_early6 = load_narrow(columns(x6, early))
-        raw_early7 = load_narrow(columns(x7, early))
-        quantize_w(c6, cast(raw_w6, 0))
-        quantize_w(c7, cast(raw_w7, 0))
-        raw_rest6 = load_wide(x6[:, N:])
-        raw_split7 = load_narrow(columns(x7, split))
-        raw_late7 = load_narrow(columns(x7, late))
+        raw = {}
+        for c in range(WHOLE, CHUNKS):
+            raw[c, early] = load_narrow(columns(c, early, early + 1))
+        rest = load_wide(columns(WHOLE, split, late + 1))
+        raw[WHOLE, split], raw[WHOLE, late] = piece(rest, 0), piece(rest, 1)
+        for c, r in ((WHOLE + 1, split), (WHOLE + 2, split), (WHOLE + 1, late)):
+            raw[c, r] = load_narrow(columns(c, r, r + 1))
 
-        quantize_x(c6, early, cast(raw_early6, V_COLS))
-        for m in range(M_TILES):
-            multiply(c6, early, m, False, False)
-        quantize_x(c7, early, cast(raw_early7, V_COLS))
-        for m in range(M_TILES):
-            multiply(c7, early, m, False, True)
-        for m in range(M_TILES):
-            finish(early, m, m % 2 == 1)
-            open_bank(split, m, 4 + m)
-            for c in range(SPILL, c6):
-                multiply(c, split, m, c == SPILL, False)
-
-        grouped_split = cast(piece(raw_rest6, 0), V_COLS)
-        grouped_late = cast(piece(raw_rest6, 1), V_COLS)
-        quantize_x(c6, split, grouped_split)
-        quantize_x(c6, late, grouped_late)
-        for r in (split, late):
+        def multiply_all(c, r):
             for m in range(M_TILES):
-                multiply(c6, r, m, False, False)
+                multiply(c, r, m, False, c == CHUNKS - 1)
 
-        quantize_x(c7, split, cast(raw_split7, V_COLS))
+        for c in range(WHOLE, CHUNKS):
+            grouped = cast(raw[c, early], V_COLS)
+            if c == WHOLE:
+                raw[CHUNKS - 1, late] = load_narrow(columns(CHUNKS - 1, late, late + 1))
+            quantize_x(c, early, grouped)
+            multiply_all(c, early)
+
         for m in range(M_TILES):
-            multiply(c7, split, m, False, True)
-        quantize_x(c7, late, cast(raw_late7, V_COLS))
+            finish(early, m, False)
+            open_bank(split, m, 4 + m)
+            for c in range(WHOLE):
+                multiply(c, split, m, c == 0, False)
+
+        c5, c6, c7 = range(WHOLE, CHUNKS)
+        grouped_split = cast(raw[c5, split], V_COLS)
+        grouped_late = cast(raw[c5, late], V_COLS)
+        quantize_x(c5, split, grouped_split)
+        multiply_all(c5, split)
+        grouped_split = cast(raw[c6, split], V_COLS)
+        quantize_x(c5, late, grouped_late)
+        quantize_x(c6, split, grouped_split)
+        multiply_all(c6, split)
+        quantize_x(c7, split, cast(raw[c7, split], V_COLS))
+        multiply_all(c7, split)
+        multiply_all(c5, late)
+
+        grouped_late = cast(raw[c6, late], V_COLS)
+        finish(split, 0, False)
+        finish(split, 1, False)
+        quantize_x(c6, late, grouped_late)
+        multiply_all(c6, late)
+        grouped_late = cast(raw[c7, late], V_COLS)
+        finish(split, 2, False)
+        finish(split, 3, False)
+        quantize_x(c7, late, grouped_late)
+        multiply_all(c7, late)
         for m in range(M_TILES):
-            multiply(c7, late, m, False, True)
-        for m in range(M_TILES):
-            finish_partial(split, m)
-        for m in range(M_TILES):
-            finish(late, m, m == M_TILES - 1)
+            finish(late, m, m % 2 == 0)

from contextlib import ExitStack

import concourse.mybir as mybir

K, M, T = 2048, 512, 1536
FLOPS = 2 * 2 * K * M * T

F32 = mybir.dt.float32
BF16 = mybir.dt.bfloat16
U32 = mybir.dt.uint32
U8 = mybir.dt.uint8
E4M3 = mybir.dt.float8_e4m3fn_x4
E5M2 = mybir.dt.float8_e5m2_x4
IDENTITY = mybir.ActivationFunctionType.Identity
ADD = mybir.AluOpType.add

P = 128
PACK = 4
K_PASS = P * PACK
N = 512
M_TILES = M // P
RANGES = T // N
CHUNKS = 2 * K // K_PASS
WHOLE = 5
V_COLS = 336


def tile_mix_jvp_fm_bias_kernel(tc, w, xd, wd, x, b, out):
    nc = tc.nc

    with ExitStack() as ctx:
        const = ctx.enter_context(tc.tile_pool(name="const", bufs=1))
        wide = ctx.enter_context(tc.tile_pool(name="wide", bufs=2))
        narrow = ctx.enter_context(tc.tile_pool(name="narrow", bufs=6))
        group = ctx.enter_context(tc.tile_pool(name="group", bufs=6))
        banks = ctx.enter_context(tc.psum_pool(name="banks", bufs=1))
        ctx.enter_context(tc.manual_schedule())

        w_codes = const.tile([P, CHUNKS, M], U32, align_bytes=64)
        w_scales = const.tile([P, CHUNKS, M], U8, align_bytes=64)
        x_codes = const.tile([P, CHUNKS, RANGES, N], U32, align_bytes=64)
        x_scales = const.tile([P, CHUNKS, RANGES, N], U8, align_bytes=64)
        results = const.tile([P, RANGES, M_TILES, N], F32, align_bytes=64)
        bias_rows = const.tile([P, 32], F32, align_bytes=64)
        bias = const.tile([P, 32], F32, align_bytes=64)

        def operands(c):
            g = c // 2
            rows = slice(g * K_PASS, (g + 1) * K_PASS)
            if c % 2 == 0:
                return w[rows, :], E4M3, xd[rows, :], E5M2
            return wd[rows, :], E5M2, x[rows, :], E4M3

        def load_narrow(src):
            raw = narrow.tile([P, PACK, N], F32, name="raw", align_bytes=64)
            nc.sync.dma_start(out=raw[:], in_=src.rearrange("(p j) c -> p j c", j=PACK))
            return raw

        def load_wide(src):
            raw_wide = wide.tile([P, PACK, src.shape[1]], F32, name="raw_wide", align_bytes=64)
            nc.sync.dma_start(out=raw_wide[:], in_=src.rearrange("(p j) c -> p j c", j=PACK))
            return raw_wide

        def interleave(copy, grouped, raw, c0, c1):
            copy(
                out=grouped[:, c0:c1, :].rearrange("p (c i) t -> p c t i", i=4),
                in_=raw[:, :, c0:c1].rearrange("p t (c i) -> p c t i", i=4),
            )

        def cast(raw, v_cols):
            grouped = group.tile([P, N, PACK], BF16, name="grouped", align_bytes=64)
            if v_cols < N:
                interleave(nc.scalar.copy, grouped, raw, v_cols, N)
            if v_cols > 0:
                interleave(nc.vector.tensor_copy, grouped, raw, 0, v_cols)
            return grouped

        def quantize(grouped, codes, scales, fmt):
            nc.vector.quantize_mx(
                out=codes.bitcast(fmt), scales=scales, in_=grouped[:].rearrange("p c t -> p (c t)")
            )

        def quantize_w(c, grouped):
            quantize(grouped, w_codes[:, c, :], w_scales[:, c, :], operands(c)[1])

        def quantize_x(c, r, grouped):
            quantize(grouped, x_codes[:, c, r, :], x_scales[:, c, r, :], operands(c)[3])

        acc = {}

        def open_bank(r, m, bank):
            acc[r, m] = banks.tile([P, N], F32, name="bank" + str(bank))

        def multiply(c, r, m, start, stop):
            cols = slice(m * P, (m + 1) * P)
            nc.tensor.matmul_mx(
                out=acc[r, m][:],
                lhsT=w_codes[:, c, cols].bitcast(operands(c)[1]),
                lhsT_scale=w_scales[:, c, cols],
                rhs=x_codes[:, c, r, :].bitcast(operands(c)[3]),
                rhs_scale=x_scales[:, c, r, :],
                start=start,
                stop=stop,
            )

        def add_bias(r, m, on_vector):
            if on_vector:
                nc.vector.tensor_scalar(
                    out=results[:, r, m, :], in0=acc[r, m][:], scalar1=bias[:, m : m + 1], scalar2=None, op0=ADD
                )
            else:
                nc.scalar.activation(
                    out=results[:, r, m, :], in_=acc[r, m][:], func=IDENTITY, bias=bias[:, m : m + 1]
                )

        def store(r, m):
            nc.sync.dma_start(out=out[m * P : (m + 1) * P, r * N : (r + 1) * N], in_=results[:, r, m, :])

        nc.vector.memset(bias_rows[:], 0.0)
        for m in range(M_TILES):
            nc.scalar.dma_start(
                out=bias_rows[m : P : 32, :], in_=b[m * P : (m + 1) * P].rearrange("(q i) -> q i", i=32)
            )

        def finish(r, m, on_vector):
            add_bias(r, m, on_vector)
            store(r, m)

        def piece(raw, i):
            return raw[:, :, i * N : (i + 1) * N]

        early, split, late = 0, 1, 2
        AHEAD = 3
        raw_w = [load_narrow(operands(c)[0]) for c in range(AHEAD)]
        for c in range(WHOLE):
            raw_w.append(load_narrow(operands(c + AHEAD)[0]))
            raw_x = load_wide(operands(c)[2])
            for ready in range(0 if c == 0 else c + AHEAD, c + AHEAD + 1):
                quantize_w(ready, cast(raw_w[ready], 0))
            grouped_x = [cast(piece(raw_x, 0), V_COLS), cast(piece(raw_x, 1), V_COLS)]
            quantize_x(c, 0, grouped_x[0])
            grouped_x.append(cast(piece(raw_x, 2), V_COLS))
            quantize_x(c, 1, grouped_x[1])
            quantize_x(c, 2, grouped_x[2])
            for r, bank in ((late, 0), (early, 4)):
                for m in range(M_TILES):
                    if c == 0:
                        open_bank(r, m, bank + m)
                    multiply(c, r, m, c == 0, False)

        nc.vector.transpose(bias[:], bias_rows[:])

        def columns(c, r0, r1):
            return operands(c)[2][:, r0 * N : r1 * N]

        raw = {}
        for c in range(WHOLE, CHUNKS):
            raw[c, early] = load_narrow(columns(c, early, early + 1))
        rest = load_wide(columns(WHOLE, split, late + 1))
        raw[WHOLE, split], raw[WHOLE, late] = piece(rest, 0), piece(rest, 1)
        for c, r in ((WHOLE + 1, split), (WHOLE + 2, split), (WHOLE + 1, late)):
            raw[c, r] = load_narrow(columns(c, r, r + 1))

        def multiply_all(c, r):
            for m in range(M_TILES):
                multiply(c, r, m, False, c == CHUNKS - 1)

        for c in range(WHOLE, CHUNKS):
            grouped = cast(raw[c, early], V_COLS)
            if c == WHOLE:
                raw[CHUNKS - 1, late] = load_narrow(columns(CHUNKS - 1, late, late + 1))
            quantize_x(c, early, grouped)
            multiply_all(c, early)

        for m in range(M_TILES):
            finish(early, m, False)
            open_bank(split, m, 4 + m)
            for c in range(WHOLE):
                multiply(c, split, m, c == 0, False)

        c5, c6, c7 = range(WHOLE, CHUNKS)
        grouped_split = cast(raw[c5, split], V_COLS)
        grouped_late = cast(raw[c5, late], V_COLS)
        quantize_x(c5, split, grouped_split)
        multiply_all(c5, split)
        grouped_split = cast(raw[c6, split], V_COLS)
        quantize_x(c5, late, grouped_late)
        quantize_x(c6, split, grouped_split)
        multiply_all(c6, split)
        quantize_x(c7, split, cast(raw[c7, split], V_COLS))
        multiply_all(c7, split)
        multiply_all(c5, late)

        grouped_late = cast(raw[c6, late], V_COLS)
        finish(split, 0, False)
        finish(split, 1, False)
        quantize_x(c6, late, grouped_late)
        multiply_all(c6, late)
        grouped_late = cast(raw[c7, late], V_COLS)
        finish(split, 2, False)
        finish(split, 3, False)
        quantize_x(c7, late, grouped_late)
        multiply_all(c7, late)
        for m in range(M_TILES):
            finish(late, m, m % 2 == 0)
